import numpy as np, ml_dtypes
CORES = [2,7,18,23,34]
N = 5
import mx_ref
BF = ml_dtypes.bfloat16
def gentries(a):
    return np.ascontiguousarray(a.reshape(8, 16, -1).transpose(0, 2, 1)).reshape(8, -1)
def gtable(e):
    e = np.asarray(e); return np.ascontiguousarray(e.reshape(8, -1, 16).transpose(0, 2, 1)).reshape(128, -1).astype(np.int32)
def gcols(t, e):
    v = np.concatenate([t.reshape(8, 16, -1, 4), np.zeros((8, 16, 1, 4), BF)], axis=2)
    return np.ascontiguousarray(np.stack([v[g][:, e[g]] for g in range(8)])).reshape(128, -1)
def f(rng, *shape):
    return mx_ref.flush((rng.standard_normal(shape, dtype=np.float32) * np.exp2(rng.integers(-2, 3, shape[:-1] + (1,)))).astype(BF))
def wide(rng, *shape, cols=0):
    v = rng.standard_normal(shape, dtype=np.float32) * np.exp2(rng.integers(-12, 13, shape)).astype(np.float32)
    if cols: v *= np.repeat(np.exp2(rng.integers(-cols, cols + 1, shape[:-2] + (1, shape[-1] // 4))) * (rng.random(shape[:-2] + (1, shape[-1] // 4)) > 0.0625), 4, axis=-1).astype(np.float32)
    return mx_ref.flush(v.astype(BF))
T, O, K = 128, 4, 256
def lists(rng, alike=False, groups=False, ends=False, few=False):
    c = []
    for r in range(N):
        e = rng.integers(0, K, (8, O, 2, 128))
        if groups: e = np.stack([e[0]] * 8)
        if ends: e = rng.permuted(np.resize([0, K - 1], (8, O, 2, 128)), axis=3)
        if few:
            for m in range(2): e[:, :, m] = rng.permutation(np.resize(rng.permutation(K)[:8], 8 * O * 128)).reshape(8, O, 128)
        c.append(gtable(e.reshape(8, -1)))
    if alike: c = [c[0]] * N
    return np.stack(c)
def setup_inputs(rng):
    return {"x": f(rng, N, 128, 4 * T), "book": np.stack([f(rng, 128, 8 * K)] * N), "cw": lists(rng)}
def setup_inputs_alike(rng):
    d = setup_inputs(rng); d["cw"] = lists(rng, alike=True); return d
def setup_inputs_groups(rng):
    d = setup_inputs(rng); d["cw"] = lists(rng, groups=True); return d
def setup_inputs_ends(rng):
    d = setup_inputs(rng); d["cw"] = lists(rng, ends=True); return d
def setup_inputs_few(rng):
    d = setup_inputs(rng); d["cw"] = lists(rng, few=True); return d
def setup_inputs_spread(rng):
    d = setup_inputs(rng); d["x"] = wide(rng, N, 128, 4 * T, cols=8); d["book"] = np.stack([wide(rng, 128, 8 * K, cols=4)] * N); return d
def check_inputs(d):
    b = []
    for r in range(N):
        if d["cw"][r].min() < 0 or d["cw"][r].max() >= K: b.append("cw")
        if d["book"][r].tobytes() != d["book"][0].tobytes(): b.append("book")
    return b
def reference(x, book, cw):
    W = []
    for s in range(N):
        e = gentries(cw[s])
        for o in range(O):
            a, b = [gcols(np.ascontiguousarray(book[s][:, 4 * K * m:4 * K * m + 4 * K]), e[:, (2 * o + m) * 128:(2 * o + m) * 128 + 128]).astype(np.float32) for m in range(2)]
            W.append(mx_ref.quantize((a + b).astype(BF)))
    y = np.zeros((N, 128, N * O * T), np.float32)
    for r in range(N):
        X = mx_ref.quantize(np.ascontiguousarray(x[r]))
        for i in range(N * O): y[r][:, T * i:T * i + T] = mx_ref.matmul(W[i], X)
    return {"y": y}

@@ -1,0 +1,238 @@
+from concourse.bass import DstId, RemoteDMATransfer
+from concourse.mybir import dt, AluOpType, ActivationFunctionType
+
+NR, O, TC = 5, 4, 128
+NB = 2 * NR
+BC = 2 * TC
+LC = 2 * BC // 16
+
+MAKE = [[0, 1, 5, 9], [2, 3, 7, 9], [4, 5, 1, 9], [6, 7, 3, 9], [8, 9, 3, 5]]
+SEND = [
+    {0: [1, 2, 3, 4], 1: [1, 4], 5: [1]},
+    {2: [0, 2, 3, 4], 3: [0], 7: [0]},
+    {4: [3, 0, 1, 4], 5: [3], 1: [3]},
+    {6: [2, 0, 1, 4], 7: [2, 4], 3: [2]},
+    {8: [0, 1, 2, 3]},
+]
+ORDER = [
+    [0, 1, 2, 5, 3, 9, 4, 6, 7, 8],
+    [2, 3, 0, 7, 1, 9, 6, 4, 5, 8],
+    [4, 5, 6, 1, 7, 9, 0, 2, 3, 8],
+    [6, 7, 4, 3, 5, 9, 2, 0, 1, 8],
+    [8, 9, 3, 5, 0, 2, 4, 6, 1, 7],
+]
+COPY = [{1: [0], 2: [1, 2], 3: [5, 3]}, {1: [2], 2: [3, 0], 3: [7, 1]}, {1: [4], 2: [5, 6], 3: [1, 7]},
+        {1: [6], 2: [7, 4], 3: [3, 5]}, {1: [8], 2: [9], 3: [3]}]
+NM = 4
+NF = 2
+
+SCRATCH = {
+    "cws": ("sbuf", [128, 64], "int32"),
+    "bk0": ("sbuf", [128, 1024], "bfloat16"),
+    "bk1": ("sbuf", [128, 1024], "bfloat16"),
+    "xs": ("sbuf", [128, 4 * TC], "bfloat16"),
+    "xq": ("sbuf", [128, TC], "float8_e4m3fn_x4"),
+    "xsc": ("sbuf", [128, TC], "uint8"),
+    "wq": ("sbuf", [128, NB * BC], "float8_e4m3fn_x4"),
+    "wsc": ("sbuf", [128, NB * BC], "uint8"),
+    "ys": ("sbuf", [128, NB * BC], "float32"),
+    "ps": ("psum", [128, 512 * 8], "float32"),
+}
+for _t in range(4):
+    SCRATCH["off%d" % _t] = ("sbuf", [128, 2 * LC], "uint16")
+    SCRATCH["lof%d" % _t] = ("sbuf", [128, NF * LC], "uint16")
+for _k in range(NM):
+    SCRATCH["tmp%d" % _k] = ("sbuf", [128, 4 * BC], "bfloat16")
+    SCRATCH["w%d" % _k] = ("sbuf", [128, 4 * BC], "bfloat16")
+
+SEMAPHORES = ["ldc", "ldb0", "ldb1", "ldx", "idx", "lidx", "sg", "vw", "vq", "xqd", "mm", "cps", "cpv", "st", "loc"]
+SEMAPHORES += ["arr%d" % _b for _b in range(NB)] + ["larr%d" % _b for _b in range(NB)]
+
+
+def bits(engs):
+    return sum(1 << e for e in engs)
+
+
+def code_groups(r, batch, T, topo):
+    me = T.cores[r]
+    dst = SEND[r].get(batch, [])
+    near = [d for d in dst if topo.chip(T.cores[d]) == topo.chip(me)]
+    far = [d for d in dst if d not in near]
+    out, fe = [], []
+    if far:
+        fe = topo.engines(me, T.cores[far[0]])
+        out.append((fe, far))
+    if near:
+        out.append(([e for e in topo.engines(me, T.cores[near[0]]) if e not in fe], near))
+    return out
+
+
+def rank_program(g, core, T, topo):
+    r = T.rank_of(core)
+    if r is None:
+        return
+    S = T.sem
+    V, A, P = g.vector, g.scalar, g.tensor
+    copy = ActivationFunctionType.Copy
+    make, order = MAKE[r], ORDER[r]
+    foreign = [b for b in make if b // 2 != r]
+
+    def dst_of(d):
+        rid, pid, _se = topo.addr(T.cores[d])
+        return DstId(rid=rid, pnc=pid)
+
+    def lists_of(k, t):
+        b = make[k]
+        if b // 2 == r:
+            return T["off%d" % t], (b % 2) * LC
+        return T["lof%d" % t], foreign.index(b) * LC
+
+    g.sync.dma_start(T.cws[:], T.cw[:, :]).then_inc(S.ldc, 16)
+    A.dma_start(T.bk0[:], T.book[:, 0:1024]).then_inc(S.ldb0, 16)
+    g.sync.dma_start(T.bk1[:], T.book[:, 1024:2048]).then_inc(S.ldb1, 16)
+    A.dma_start(T.xs[:], T.x[:, :]).then_inc(S.ldx, 16)
+
+    V.wait_ge(S.ldc, 16)
+    for h in (1, 0):
+        for m in range(2):
+            for i in range(2):
+                src = (2 * (2 * h + i) + m) * 8
+                to = h * LC + m * (LC // 2) + i * 8
+                V.tensor_scalar(T.off0[:, to:to + 8], T.cws[:, src:src + 8], 4, None, AluOpType.mult).then_inc(S.idx, 1)
+    V.wait_ge(S.idx, 8)
+    for t in range(1, 4):
+        V.tensor_scalar(T["off%d" % t][:], T.off0[:], t, None, AluOpType.add).then_inc(S.idx, 1)
+
+    loc = 0
+    tr = []
+    asks = {}
+    for d in range(NR):
+        for b in MAKE[d]:
+            if b // 2 == r and d != r:
+                asks.setdefault(b, []).append(d)
+    for b in sorted(asks):
+        engs = topo.engines(core, T.cores[asks[b][0]])
+        at = (b % 2) * LC
+        dsts = []
+        for d in asks[b]:
+            f = [q for q in MAKE[d] if q // 2 != d].index(b)
+            dsts.append(T.lof0[:, f * LC:(f + 1) * LC])
+        tr.append(RemoteDMATransfer(dst_ids=[dst_of(d) for d in asks[b]], dma_engine_mask=bits(engs),
+                                    remote_sem=S["larr%d" % b], srcs=[T.off0[:, at:at + LC]], dsts=dsts))
+        loc += len(engs)
+    if tr:
+        g.wait_ge(S.idx, 4)
+        g.remote_dma_fused(tr, local_sem=S.loc)
+
+    def list_engines(b):
+        return len(topo.engines(T.cores[b // 2], core))
+
+    where = {}
+    ncp = {"s": 0, "v": 0}
+
+    def copy_out(i, eng):
+        b, h = order[i // 2], i % 2
+        bank = (i % 8) * 512
+        to = b * BC + h * TC
+        ncp[eng] += 1
+        if eng == "s":
+            A.wait_ge(S.mm, i + 1)
+            A.activation(T.ys[:, to:to + TC], T.ps[:, bank:bank + TC], copy).then_inc(S.cps, 1)
+            where[i] = (S.cps, ncp[eng])
+        else:
+            V.wait_ge(S.mm, i + 1)
+            V.tensor_copy(T.ys[:, to:to + TC], T.ps[:, bank:bank + TC]).then_inc(S.cpv, 1)
+            where[i] = (S.cpv, ncp[eng])
+
+    def foreign_offsets():
+        for b in foreign:
+            V.wait_ge(S["larr%d" % b], list_engines(b))
+        for t in range(1, 4):
+            V.tensor_scalar(T["lof%d" % t][:], T.lof0[:], t, None, AluOpType.add).then_inc(S.lidx, 1)
+
+    done = []
+    for k in range(NM):
+        far_list = make[k] // 2 != r
+        if k == 0:
+            A.wait_ge(S.ldb0, 16)
+        for t in range(4):
+            if far_list:
+                if t == 0:
+                    A.wait_ge(S["larr%d" % make[k]], list_engines(make[k]))
+                elif k == NM - NF:
+                    A.wait_ge(S.lidx, t)
+            elif k == 0:
+                A.wait_ge(S.idx, 8 + t)
+            buf, at = lists_of(k, t)
+            A.activation(T["tmp%d" % k][:, t * BC:(t + 1) * BC],
+                         T.bk0[:, 0:1024].indirect(buf[:, at:at + LC // 2]), copy).then_inc(S.sg, 1)
+        for b in COPY[r].get(k, []):
+            for h in range(2):
+                i = 2 * order.index(b) + h
+                copy_out(i, "s")
+                done.append(i)
+
+    for k in range(NM):
+        for t in range(4):
+            if k == 0 and t == 0:
+                V.wait_ge(S.idx, 11)
+                V.wait_ge(S.ldb1, 16)
+            if k == NM - NF and t == 0:
+                V.wait_ge(S.lidx, 3)
+            V.wait_ge(S.sg, 4 * k + t + 1)
+            buf, at = lists_of(k, t)
+            V.tensor_tensor(T["w%d" % k][:, t:4 * BC:4],
+                            T.bk1[:, 0:1024].indirect(buf[:, at + LC // 2:at + LC]),
+                            T["tmp%d" % k][:, t * BC:(t + 1) * BC], AluOpType.add).then_inc(S.vw, 1)
+            if k == NM - NF - 1 and t == 2:
+                foreign_offsets()
+        V.wait_ge(S.vw, 4 * (k + 1))
+        c = make[k] * BC
+        V.quantize_mx(T.wq[:, c:c + BC], T.wsc[:, c:c + BC], T["w%d" % k][:]).then_inc(S.vq, 1)
+        if k == 0:
+            V.wait_ge(S.ldx, 16)
+            V.quantize_mx(T.xq[:], T.xsc[:], T.xs[:]).then_inc(S.xqd, 1)
+
+    rest = [i for i in range(2 * NB) if i not in done]
+    for n, i in enumerate(rest):
+        copy_out(i, "sv"[n % 2])
+
+    P.wait_ge(S.xqd, 1)
+    for j, b in enumerate(order):
+        if b in make:
+            P.wait_ge(S.vq, make.index(b) + 1)
+        else:
+            n = 0
+            for s in range(NR):
+                if r in SEND[s].get(b, []):
+                    n += sum(2 * len(e) for e, dd in code_groups(s, b, T, topo) if r in dd)
+            P.wait_ge(S["arr%d" % b], n)
+        for h in range(2):
+            i = 2 * j + h
+            if i >= 8:
+                P.wait_ge(where[i - 8][0], where[i - 8][1])
+            c = b * BC + h * TC
+            bank = (i % 8) * 512
+            P.matmul_mx(T.ps[:, bank:bank + TC], T.wq[:, c:c + TC], T.wsc[:, c:c + TC], T.xq[:], T.xsc[:],
+                        True, True).then_inc(S.mm, 1)
+
+    for j, b in enumerate(order):
+        for h in range(2):
+            g.sync.wait_ge(where[2 * j + h][0], where[2 * j + h][1])
+        g.sync.dma_start(T.y[:, b * BC:(b + 1) * BC], T.ys[:, b * BC:(b + 1) * BC]).then_inc(S.st, 16)
+    g.sync.wait_ge(S.st, 16 * NB)
+
+    for k, b in enumerate(make):
+        grp = code_groups(r, b, T, topo)
+        if not grp:
+            continue
+        g.wait_ge(S.vq, k + 1)
+        c = b * BC
+        for src in (T.wq[:, c:c + BC].bitcast(dt.uint8), T.wsc[:, c:c + BC]):
+            tr = []
+            for engs, dd in grp:
+                tr.append(RemoteDMATransfer(dst_ids=[dst_of(d) for d in dd], dma_engine_mask=bits(engs),
+                                            remote_sem=S["arr%d" % b], srcs=[src], dsts=[src] * len(dd)))
+                loc += len(engs)
+            g.remote_dma_fused(tr, local_sem=S.loc)
+    g.wait_ge(S.loc, loc)

@@ -2,138 +2,198 @@ from concourse.bass import DstId, RemoteDMATransfer
 from concourse.mybir import dt, AluOpType, ActivationFunctionType
 
 NR, O, TC = 5, 4, 128
-NB = 2 * NR
-BC = 2 * TC
-LC = 2 * BC // 16
-
-MAKE = [[0, 1, 5, 9], [2, 3, 7, 9], [4, 5, 1, 9], [6, 7, 3, 9], [8, 9, 3, 5]]
-SEND = [
-    {0: [1, 2, 3, 4], 1: [1, 4], 5: [1]},
-    {2: [0, 2, 3, 4], 3: [0], 7: [0]},
-    {4: [3, 0, 1, 4], 5: [3], 1: [3]},
-    {6: [2, 0, 1, 4], 7: [2, 4], 3: [2]},
-    {8: [0, 1, 2, 3]},
-]
-ORDER = [
-    [0, 1, 2, 5, 3, 9, 4, 6, 7, 8],
-    [2, 3, 0, 7, 1, 9, 6, 4, 5, 8],
-    [4, 5, 6, 1, 7, 9, 0, 2, 3, 8],
-    [6, 7, 4, 3, 5, 9, 2, 0, 1, 8],
-    [8, 9, 3, 5, 0, 2, 4, 6, 1, 7],
-]
-COPY = [{1: [0], 2: [1, 2], 3: [5, 3]}, {1: [2], 2: [3, 0], 3: [7, 1]}, {1: [4], 2: [5, 6], 3: [1, 7]},
-        {1: [6], 2: [7, 4], 3: [3, 5]}, {1: [8], 2: [9], 3: [3]}]
-NM = 4
-NF = 2
+NT = NR * O
+LW = TC // 16
+NM, NF, NG = 6, 2, 3
+RUNS = [(0,), (1,), (2,)]
+DIRECT = 1
+HOP_NEAR, HOP_FAR, HOP_HOME, HOP_TWO = 1.7, 2.5, 3.2, 3.7
+S_COPIES = {2: 1, 3: 1, 4: 2, 5: 8}
 
 SCRATCH = {
-    "cws": ("sbuf", [128, 64], "int32"),
+    "cws": ("sbuf", [128, 2 * O, LW], "int32"),
+    "off": ("sbuf", [128, 2 * O, 4 * LW], "uint16"),
+    "snd": ("sbuf", [128, 2, 2 * LW], "uint16"),
+    "lof": ("sbuf", [128, 2 * NF, 2 * LW], "uint16"),
+    "lof2": ("sbuf", [128, 2 * NF, 2 * LW], "uint16"),
     "bk0": ("sbuf", [128, 1024], "bfloat16"),
     "bk1": ("sbuf", [128, 1024], "bfloat16"),
     "xs": ("sbuf", [128, 4 * TC], "bfloat16"),
     "xq": ("sbuf", [128, TC], "float8_e4m3fn_x4"),
     "xsc": ("sbuf", [128, TC], "uint8"),
-    "wq": ("sbuf", [128, NB * BC], "float8_e4m3fn_x4"),
-    "wsc": ("sbuf", [128, NB * BC], "uint8"),
-    "ys": ("sbuf", [128, NB * BC], "float32"),
+    "wq": ("sbuf", [128, NT * TC], "float8_e4m3fn_x4"),
+    "wsc": ("sbuf", [128, NT * TC], "uint8"),
+    "ys": ("sbuf", [128, NT * TC], "float32"),
     "ps": ("psum", [128, 512 * 8], "float32"),
 }
-for _t in range(4):
-    SCRATCH["off%d" % _t] = ("sbuf", [128, 2 * LC], "uint16")
-    SCRATCH["lof%d" % _t] = ("sbuf", [128, NF * LC], "uint16")
 for _k in range(NM):
-    SCRATCH["tmp%d" % _k] = ("sbuf", [128, 4 * BC], "bfloat16")
-    SCRATCH["w%d" % _k] = ("sbuf", [128, 4 * BC], "bfloat16")
+    SCRATCH["tmp%d" % _k] = ("sbuf", [128, 4 * TC], "bfloat16")
+    SCRATCH["w%d" % _k] = ("sbuf", [128, 4 * TC], "bfloat16")
 
-SEMAPHORES = ["ldc", "ldb0", "ldb1", "ldx", "idx", "lidx", "sg", "vw", "vq", "xqd", "mm", "cps", "cpv", "st", "loc"]
-SEMAPHORES += ["arr%d" % _b for _b in range(NB)] + ["larr%d" % _b for _b in range(NB)]
+SEMAPHORES = ["ldc", "ldb0", "ldb1", "ldx", "idx", "sidx", "lidx", "sg", "vw", "vq", "xqd", "mm", "cps", "cpv", "st",
+              "loc", "larr"]
+SEMAPHORES += ["c%d" % _t for _t in range(NT)] + ["s%d" % _t for _t in range(NT)]
 
 
 def bits(engs):
     return sum(1 << e for e in engs)
 
 
-def code_groups(r, batch, T, topo):
-    me = T.cores[r]
-    dst = SEND[r].get(batch, [])
-    near = [d for d in dst if topo.chip(T.cores[d]) == topo.chip(me)]
-    far = [d for d in dst if d not in near]
-    out, fe = [], []
-    if far:
-        fe = topo.engines(me, T.cores[far[0]])
-        out.append((fe, far))
-    if near:
-        out.append(([e for e in topo.engines(me, T.cores[near[0]]) if e not in fe], near))
-    return out
+def plan(T, topo):
+    C = list(T.cores)
+    peer = {r: [q for q in range(NR) if q != r and topo.chip(C[q]) == topo.chip(C[r])] for r in range(NR)}
+    lone = [r for r in range(NR) if not peer[r]][0]
+    pairs = [r for r in range(NR) if peer[r]]
+    peer = {r: peer[r][0] for r in pairs}
+    twin = {r: [q for q in pairs if topo.chip(C[q]) != topo.chip(C[r]) and topo.die(C[q]) == topo.die(C[r])][0]
+            for r in pairs}
+    taken = set(C)
+
+    def spare(near, die):
+        c = [c for c in topo.cores_of(near) if c not in taken and topo.die(c) == die][0]
+        taken.add(c)
+        return c
+
+    a, b = pairs[0], twin[pairs[0]]
+    gets = [a, peer[b]]
+    last = lambda r: O * r + O - 1
+    slots = [O * r + o for r in range(NR) for o in range(NG)] + [last(r) for r in (a, b, peer[a], peer[b], lone)]
+    place = {t: i for i, t in enumerate(slots)}
+    make, sends = {}, {}
+    late = {r: {} for r in range(NR)}
+
+    def call(core, items):
+        far = [(run, [c for c in cs if topo.chip(c) != topo.chip(core)]) for run, cs in items]
+        near = [(run, [c for c in cs if topo.chip(c) == topo.chip(core)]) for run, cs in items]
+        far, near = [x for x in far if x[1]], [x for x in near if x[1]]
+        out = topo.engines(core, [c for c in C if topo.chip(c) != topo.chip(core)][0])
+        tr = []
+        for group in (far, near):
+            if group:
+                engs = topo.engines(core, group[0][1][0])
+                if group is near and (far or core in C):
+                    engs = [e for e in engs if e not in out]
+                n = len(engs) // len(group)
+                tr += [(sorted(run, key=place.get), cs, engs[i * n:(i + 1) * n]) for i, (run, cs) in enumerate(group)]
+        sends.setdefault(core, []).append(tr)
+
+    def expect(ranks, run, when):
+        for d in ranks:
+            for t in run:
+                late[d][t] = when
+
+    for r in pairs:
+        make[r] = [O * r + o for o in range(O)] + [last(twin[r]), last(lone)]
+        h = spare(C[twin[r]], topo.die(C[r]))
+        home = spare(C[r], topo.die(C[r]))
+        for ks in RUNS:
+            run = [make[r][k] for k in ks]
+            direct = ks[-1] < DIRECT
+            call(C[r], [(run, [home, h] + [C[lone]] * direct)])
+            call(home, [(run, [C[peer[r]]] + [C[lone]] * (not direct))])
+            call(h, [(run, [C[twin[r]]]), (run, [C[peer[twin[r]]]])])
+            expect([peer[r]], run, ks[-1] + HOP_HOME)
+            expect([twin[r], peer[twin[r]]], run, ks[-1] + HOP_TWO)
+            expect([lone], run, ks[-1] + (HOP_FAR if direct else HOP_TWO))
+        for k in (NG, NG + 1):
+            run, far = make[r][k:k + 1], [lone] if k == NG and r in gets else []
+            call(C[r], [(run, [C[peer[r]]] + [C[d] for d in far])])
+            expect([peer[r]], run, k + HOP_NEAR)
+            expect(far, run, k + HOP_FAR)
+    make[lone] = [O * lone + o for o in range(O)] + [last(r) for r in pairs if r not in gets]
+    h = spare(C[a], topo.die(C[lone]))
+    hb = {d: spare(C[lone], topo.die(C[d])) for d in (b, peer[b])}
+    for ks in RUNS:
+        run = [make[lone][k] for k in ks]
+        call(C[lone], [(run, [h] + list(hb.values()))])
+        call(h, [(run, [C[a], C[peer[a]]])])
+        for d in hb:
+            call(hb[d], [(run, [C[d]])])
+        expect(pairs, run, ks[-1] + HOP_TWO)
+    for r in range(NR):
+        for k, t in enumerate(make[r]):
+            late[r][t] = k
+    return make, place, sends, late
 
 
 def rank_program(g, core, T, topo):
-    r = T.rank_of(core)
-    if r is None:
-        return
     S = T.sem
-    V, A, P = g.vector, g.scalar, g.tensor
-    copy = ActivationFunctionType.Copy
-    make, order = MAKE[r], ORDER[r]
-    foreign = [b for b in make if b // 2 != r]
+    make_all, place, sends, late = plan(T, topo)
+    r = T.rank_of(core)
+    if r is None and core not in sends:
+        return
 
-    def dst_of(d):
-        rid, pid, _se = topo.addr(T.cores[d])
+    def dst_of(c):
+        rid, pid, _se = topo.addr(c)
         return DstId(rid=rid, pnc=pid)
 
-    def lists_of(k, t):
-        b = make[k]
-        if b // 2 == r:
-            return T["off%d" % t], (b % 2) * LC
-        return T["lof%d" % t], foreign.index(b) * LC
+    comes = {t: (run[0], len(engs)) for c in sends for tr in sends[c] for run, cs, engs in tr if core in cs for t in run}
+
+    def send_tiles(ready):
+        n = 0
+        for transfers in sends.get(core, []):
+            for kind in "sc":
+                tr = []
+                for run, cs, engs in transfers:
+                    ready(run, kind)
+                    lo, hi = place[run[0]] * TC, (place[run[-1]] + 1) * TC
+                    src = T.wsc[:, lo:hi] if kind == "s" else T.wq[:, lo:hi].bitcast(dt.uint8)
+                    tr.append(RemoteDMATransfer(dst_ids=[dst_of(d) for d in cs], dma_engine_mask=bits(engs),
+                                                remote_sem=S["%s%d" % (kind, run[0])], srcs=[src], dsts=[src] * len(cs)))
+                    n += len(engs)
+                g.remote_dma_fused(tr, local_sem=S.loc)
+        return n
+
+    seen = set()
+
+    def once(queue, name, count):
+        if (queue, name, count) not in seen:
+            seen.add((queue, name, count))
+            {"g": g, "p": g.tensor}[queue].wait_ge(S[name], count)
+
+    if r is None:
+        n = send_tiles(lambda run, kind: once("g", "%s%d" % (kind, comes[run[0]][0]), comes[run[0]][1]))
+        g.wait_ge(S.loc, n)
+        return
+
+    V, A, P = g.vector, g.scalar, g.tensor
+    copy = ActivationFunctionType.Copy
+    make = make_all[r]
+    order = sorted(range(NT), key=lambda t: (late[r][t], t))
 
     g.sync.dma_start(T.cws[:], T.cw[:, :]).then_inc(S.ldc, 16)
     A.dma_start(T.bk0[:], T.book[:, 0:1024]).then_inc(S.ldb0, 16)
     g.sync.dma_start(T.bk1[:], T.book[:, 1024:2048]).then_inc(S.ldb1, 16)
-    A.dma_start(T.xs[:], T.x[:, :]).then_inc(S.ldx, 16)
+    g.sync.dma_start(T.xs[:], T.x[:, :]).then_inc(S.ldx, 16)
 
     V.wait_ge(S.ldc, 16)
-    for h in (1, 0):
-        for m in range(2):
-            for i in range(2):
-                src = (2 * (2 * h + i) + m) * 8
-                to = h * LC + m * (LC // 2) + i * 8
-                V.tensor_scalar(T.off0[:, to:to + 8], T.cws[:, src:src + 8], 4, None, AluOpType.mult).then_inc(S.idx, 1)
-    V.wait_ge(S.idx, 8)
-    for t in range(1, 4):
-        V.tensor_scalar(T["off%d" % t][:], T.off0[:], t, None, AluOpType.add).then_inc(S.idx, 1)
+    for t in range(4):
+        V.tensor_scalar(T.off[:, :, t * LW:(t + 1) * LW], T.cws[:], 4, t, AluOpType.mult, AluOpType.add).then_inc(S.idx, 1)
+        if t == 0:
+            for u in range(2):
+                V.tensor_scalar(T.snd[:, :, u * LW:(u + 1) * LW], T.cws[:, 2 * O - 2:2 * O, :], 4, u,
+                                AluOpType.mult, AluOpType.add).then_inc(S.sidx, 1)
 
-    loc = 0
-    tr = []
-    asks = {}
-    for d in range(NR):
-        for b in MAKE[d]:
-            if b // 2 == r and d != r:
-                asks.setdefault(b, []).append(d)
-    for b in sorted(asks):
-        engs = topo.engines(core, T.cores[asks[b][0]])
-        at = (b % 2) * LC
-        dsts = []
-        for d in asks[b]:
-            f = [q for q in MAKE[d] if q // 2 != d].index(b)
-            dsts.append(T.lof0[:, f * LC:(f + 1) * LC])
-        tr.append(RemoteDMATransfer(dst_ids=[dst_of(d) for d in asks[b]], dma_engine_mask=bits(engs),
-                                    remote_sem=S["larr%d" % b], srcs=[T.off0[:, at:at + LC]], dsts=dsts))
-        loc += len(engs)
-    if tr:
-        g.wait_ge(S.idx, 4)
-        g.remote_dma_fused(tr, local_sem=S.loc)
+    asks = [d for d in range(NR) if d != r and O * r + O - 1 in make_all[d]]
+    engs = topo.engines(core, T.cores[asks[0]])
+    slots = [make_all[d].index(O * r + O - 1) - O for d in asks]
+    g.wait_ge(S.sidx, 2)
+    g.remote_dma_fused([RemoteDMATransfer(dst_ids=[dst_of(T.cores[d]) for d in asks], dma_engine_mask=bits(engs),
+                                          remote_sem=S.larr, srcs=[T.snd[:]],
+                                          dsts=[T.lof[:, 2 * f:2 * f + 2, :] for f in slots])], local_sem=S.loc)
+    loc = len(engs)
+    lists = sum(len(topo.engines(T.cores[t // O], core)) for t in make[O:])
 
-    def list_engines(b):
-        return len(topo.engines(T.cores[b // 2], core))
+    def offsets(k, m, t, n):
+        if k < O:
+            return T.off[:, 2 * k + m, t * LW:(t + n) * LW]
+        return (T.lof, T.lof2)[t // 2][:, 2 * (k - O) + m, (t % 2) * LW:(t % 2 + n) * LW]
 
     where = {}
     ncp = {"s": 0, "v": 0}
 
     def copy_out(i, eng):
-        b, h = order[i // 2], i % 2
-        bank = (i % 8) * 512
-        to = b * BC + h * TC
+        bank, to = (i % 8) * 512, order[i] * TC
         ncp[eng] += 1
         if eng == "s":
             A.wait_ge(S.mm, i + 1)
@@ -144,95 +204,72 @@ def rank_program(g, core, T, topo):
             V.tensor_copy(T.ys[:, to:to + TC], T.ps[:, bank:bank + TC]).then_inc(S.cpv, 1)
             where[i] = (S.cpv, ncp[eng])
 
-    def foreign_offsets():
-        for b in foreign:
-            V.wait_ge(S["larr%d" % b], list_engines(b))
-        for t in range(1, 4):
-            V.tensor_scalar(T["lof%d" % t][:], T.lof0[:], t, None, AluOpType.add).then_inc(S.lidx, 1)
-
-    done = []
+    got = {}
+    nsg = done = 0
+    A.wait_ge(S.ldb0, 16)
     for k in range(NM):
-        far_list = make[k] // 2 != r
-        if k == 0:
-            A.wait_ge(S.ldb0, 16)
-        for t in range(4):
-            if far_list:
-                if t == 0:
-                    A.wait_ge(S["larr%d" % make[k]], list_engines(make[k]))
-                elif k == NM - NF:
-                    A.wait_ge(S.lidx, t)
-            elif k == 0:
-                A.wait_ge(S.idx, 8 + t)
-            buf, at = lists_of(k, t)
-            A.activation(T["tmp%d" % k][:, t * BC:(t + 1) * BC],
-                         T.bk0[:, 0:1024].indirect(buf[:, at:at + LC // 2]), copy).then_inc(S.sg, 1)
-        for b in COPY[r].get(k, []):
-            for h in range(2):
-                i = 2 * order.index(b) + h
-                copy_out(i, "s")
-                done.append(i)
+        n = 1 if k == 0 else 4 if k < O else 2
+        for t in range(0, 4, n):
+            if k == 0:
+                A.wait_ge(S.idx, t + 1)
+            if k == O:
+                A.wait_ge(*((S.larr, lists) if t == 0 else (S.lidx, 1)))
+            A.activation(T["tmp%d" % k][:, t * TC:(t + n) * TC], T.bk0[:, 0:1024].indirect(offsets(k, 0, t, n)),
+                         copy).then_inc(S.sg, 1)
+            nsg += 1
+            for u in range(t, t + n):
+                got[k, u] = nsg
+        for _ in range(S_COPIES.get(k, 0)):
+            copy_out(done, "s")
+            done += 1
 
+    V.wait_ge(S.idx, 4)
+    V.wait_ge(S.ldb1, 16)
     for k in range(NM):
         for t in range(4):
-            if k == 0 and t == 0:
-                V.wait_ge(S.idx, 11)
-                V.wait_ge(S.ldb1, 16)
-            if k == NM - NF and t == 0:
-                V.wait_ge(S.lidx, 3)
-            V.wait_ge(S.sg, 4 * k + t + 1)
-            buf, at = lists_of(k, t)
-            V.tensor_tensor(T["w%d" % k][:, t:4 * BC:4],
-                            T.bk1[:, 0:1024].indirect(buf[:, at + LC // 2:at + LC]),
-                            T["tmp%d" % k][:, t * BC:(t + 1) * BC], AluOpType.add).then_inc(S.vw, 1)
-            if k == NM - NF - 1 and t == 2:
-                foreign_offsets()
+            if t == 0 or got[k, t] != got[k, t - 1]:
+                V.wait_ge(S.sg, got[k, t])
+            if k == O and t == 2:
+                V.wait_ge(S.lidx, 1)
+            V.tensor_tensor(T["w%d" % k][:, t:4 * TC:4], T.bk1[:, 0:1024].indirect(offsets(k, 1, t, 1)),
+                            T["tmp%d" % k][:, t * TC:(t + 1) * TC], AluOpType.add).then_inc(S.vw, 1)
+        if k == O - 1:
+            V.wait_ge(S.larr, lists)
+            V.tensor_scalar(T.lof2[:], T.lof[:], 2, None, AluOpType.add).then_inc(S.lidx, 1)
         V.wait_ge(S.vw, 4 * (k + 1))
-        c = make[k] * BC
-        V.quantize_mx(T.wq[:, c:c + BC], T.wsc[:, c:c + BC], T["w%d" % k][:]).then_inc(S.vq, 1)
+        c = place[make[k]] * TC
+        V.quantize_mx(T.wq[:, c:c + TC], T.wsc[:, c:c + TC], T["w%d" % k][:]).then_inc(S.vq, 1)
         if k == 0:
             V.wait_ge(S.ldx, 16)
             V.quantize_mx(T.xq[:], T.xsc[:], T.xs[:]).then_inc(S.xqd, 1)
-
-    rest = [i for i in range(2 * NB) if i not in done]
-    for n, i in enumerate(rest):
+    for n, i in enumerate(range(done, NT)):
         copy_out(i, "sv"[n % 2])
 
     P.wait_ge(S.xqd, 1)
-    for j, b in enumerate(order):
-        if b in make:
-            P.wait_ge(S.vq, make.index(b) + 1)
+    for i, t in enumerate(order):
+        if t in make:
+            P.wait_ge(S.vq, make.index(t) + 1)
         else:
-            n = 0
-            for s in range(NR):
-                if r in SEND[s].get(b, []):
-                    n += sum(2 * len(e) for e, dd in code_groups(s, b, T, topo) if r in dd)
-            P.wait_ge(S["arr%d" % b], n)
-        for h in range(2):
-            i = 2 * j + h
-            if i >= 8:
-                P.wait_ge(where[i - 8][0], where[i - 8][1])
-            c = b * BC + h * TC
-            bank = (i % 8) * 512
-            P.matmul_mx(T.ps[:, bank:bank + TC], T.wq[:, c:c + TC], T.wsc[:, c:c + TC], T.xq[:], T.xsc[:],
-                        True, True).then_inc(S.mm, 1)
+            for kind in "sc":
+                once("p", "%s%d" % (kind, comes[t][0]), comes[t][1])
+        if i >= 8:
+            P.wait_ge(*where[i - 8])
+        c, bank = place[t] * TC, (i % 8) * 512
+        P.matmul_mx(T.ps[:, bank:bank + TC], T.wq[:, c:c + TC], T.wsc[:, c:c + TC], T.xq[:], T.xsc[:],
+                    True, True).then_inc(S.mm, 1)
 
-    for j, b in enumerate(order):
-        for h in range(2):
-            g.sync.wait_ge(where[2 * j + h][0], where[2 * j + h][1])
-        g.sync.dma_start(T.y[:, b * BC:(b + 1) * BC], T.ys[:, b * BC:(b + 1) * BC]).then_inc(S.st, 16)
-    g.sync.wait_ge(S.st, 16 * NB)
+    stores = []
+    for t in order:
+        if stores and stores[-1] == [t - 1]:
+            stores[-1].append(t)
+        else:
+            stores.append([t])
+    for run in stores:
+        for t in run:
+            g.sync.wait_ge(*where[order.index(t)])
+        lo, hi = run[0] * TC, (run[-1] + 1) * TC
+        g.sync.dma_start(T.y[:, lo:hi], T.ys[:, lo:hi]).then_inc(S.st, 16)
+    g.sync.wait_ge(S.st, 16 * len(stores))
 
-    for k, b in enumerate(make):
-        grp = code_groups(r, b, T, topo)
-        if not grp:
-            continue
-        g.wait_ge(S.vq, k + 1)
-        c = b * BC
-        for src in (T.wq[:, c:c + BC].bitcast(dt.uint8), T.wsc[:, c:c + BC]):
-            tr = []
-            for engs, dd in grp:
-                tr.append(RemoteDMATransfer(dst_ids=[dst_of(d) for d in dd], dma_engine_mask=bits(engs),
-                                            remote_sem=S["arr%d" % b], srcs=[src], dsts=[src] * len(dd)))
-                loc += len(engs)
-            g.remote_dma_fused(tr, local_sem=S.loc)
+    loc += send_tiles(lambda run, kind: once("g", "vq", max(make.index(t) for t in run) + 1))
     g.wait_ge(S.loc, loc)

from concourse.bass import DstId, RemoteDMATransfer
from concourse.mybir import dt, AluOpType, ActivationFunctionType

NR, O, TC = 5, 4, 128
NT = NR * O
LW = TC // 16
NM, NF, NG = 6, 2, 3
RUNS = [(0,), (1,), (2,)]
DIRECT = 1
HOP_NEAR, HOP_FAR, HOP_HOME, HOP_TWO = 1.7, 2.5, 3.2, 3.7
S_COPIES = {2: 1, 3: 1, 4: 2, 5: 8}

SCRATCH = {
    "cws": ("sbuf", [128, 2 * O, LW], "int32"),
    "off": ("sbuf", [128, 2 * O, 4 * LW], "uint16"),
    "snd": ("sbuf", [128, 2, 2 * LW], "uint16"),
    "lof": ("sbuf", [128, 2 * NF, 2 * LW], "uint16"),
    "lof2": ("sbuf", [128, 2 * NF, 2 * LW], "uint16"),
    "bk0": ("sbuf", [128, 1024], "bfloat16"),
    "bk1": ("sbuf", [128, 1024], "bfloat16"),
    "xs": ("sbuf", [128, 4 * TC], "bfloat16"),
    "xq": ("sbuf", [128, TC], "float8_e4m3fn_x4"),
    "xsc": ("sbuf", [128, TC], "uint8"),
    "wq": ("sbuf", [128, NT * TC], "float8_e4m3fn_x4"),
    "wsc": ("sbuf", [128, NT * TC], "uint8"),
    "ys": ("sbuf", [128, NT * TC], "float32"),
    "ps": ("psum", [128, 512 * 8], "float32"),
}
for _k in range(NM):
    SCRATCH["tmp%d" % _k] = ("sbuf", [128, 4 * TC], "bfloat16")
    SCRATCH["w%d" % _k] = ("sbuf", [128, 4 * TC], "bfloat16")

SEMAPHORES = ["ldc", "ldb0", "ldb1", "ldx", "idx", "sidx", "lidx", "sg", "vw", "vq", "xqd", "mm", "cps", "cpv", "st",
              "loc", "larr"]
SEMAPHORES += ["c%d" % _t for _t in range(NT)] + ["s%d" % _t for _t in range(NT)]


def bits(engs):
    return sum(1 << e for e in engs)


def plan(T, topo):
    C = list(T.cores)
    peer = {r: [q for q in range(NR) if q != r and topo.chip(C[q]) == topo.chip(C[r])] for r in range(NR)}
    lone = [r for r in range(NR) if not peer[r]][0]
    pairs = [r for r in range(NR) if peer[r]]
    peer = {r: peer[r][0] for r in pairs}
    twin = {r: [q for q in pairs if topo.chip(C[q]) != topo.chip(C[r]) and topo.die(C[q]) == topo.die(C[r])][0]
            for r in pairs}
    taken = set(C)

    def spare(near, die):
        c = [c for c in topo.cores_of(near) if c not in taken and topo.die(c) == die][0]
        taken.add(c)
        return c

    a, b = pairs[0], twin[pairs[0]]
    gets = [a, peer[b]]
    last = lambda r: O * r + O - 1
    slots = [O * r + o for r in range(NR) for o in range(NG)] + [last(r) for r in (a, b, peer[a], peer[b], lone)]
    place = {t: i for i, t in enumerate(slots)}
    make, sends = {}, {}
    late = {r: {} for r in range(NR)}

    def call(core, items):
        far = [(run, [c for c in cs if topo.chip(c) != topo.chip(core)]) for run, cs in items]
        near = [(run, [c for c in cs if topo.chip(c) == topo.chip(core)]) for run, cs in items]
        far, near = [x for x in far if x[1]], [x for x in near if x[1]]
        out = topo.engines(core, [c for c in C if topo.chip(c) != topo.chip(core)][0])
        tr = []
        for group in (far, near):
            if group:
                engs = topo.engines(core, group[0][1][0])
                if group is near and (far or core in C):
                    engs = [e for e in engs if e not in out]
                n = len(engs) // len(group)
                tr += [(sorted(run, key=place.get), cs, engs[i * n:(i + 1) * n]) for i, (run, cs) in enumerate(group)]
        sends.setdefault(core, []).append(tr)

    def expect(ranks, run, when):
        for d in ranks:
            for t in run:
                late[d][t] = when

    for r in pairs:
        make[r] = [O * r + o for o in range(O)] + [last(twin[r]), last(lone)]
        h = spare(C[twin[r]], topo.die(C[r]))
        home = spare(C[r], topo.die(C[r]))
        for ks in RUNS:
            run = [make[r][k] for k in ks]
            direct = ks[-1] < DIRECT
            call(C[r], [(run, [home, h] + [C[lone]] * direct)])
            call(home, [(run, [C[peer[r]]] + [C[lone]] * (not direct))])
            call(h, [(run, [C[twin[r]]]), (run, [C[peer[twin[r]]]])])
            expect([peer[r]], run, ks[-1] + HOP_HOME)
            expect([twin[r], peer[twin[r]]], run, ks[-1] + HOP_TWO)
            expect([lone], run, ks[-1] + (HOP_FAR if direct else HOP_TWO))
        for k in (NG, NG + 1):
            run, far = make[r][k:k + 1], [lone] if k == NG and r in gets else []
            call(C[r], [(run, [C[peer[r]]] + [C[d] for d in far])])
            expect([peer[r]], run, k + HOP_NEAR)
            expect(far, run, k + HOP_FAR)
    make[lone] = [O * lone + o for o in range(O)] + [last(r) for r in pairs if r not in gets]
    h = spare(C[a], topo.die(C[lone]))
    hb = {d: spare(C[lone], topo.die(C[d])) for d in (b, peer[b])}
    for ks in RUNS:
        run = [make[lone][k] for k in ks]
        call(C[lone], [(run, [h] + list(hb.values()))])
        call(h, [(run, [C[a], C[peer[a]]])])
        for d in hb:
            call(hb[d], [(run, [C[d]])])
        expect(pairs, run, ks[-1] + HOP_TWO)
    for r in range(NR):
        for k, t in enumerate(make[r]):
            late[r][t] = k
    return make, place, sends, late


def rank_program(g, core, T, topo):
    S = T.sem
    make_all, place, sends, late = plan(T, topo)
    r = T.rank_of(core)
    if r is None and core not in sends:
        return

    def dst_of(c):
        rid, pid, _se = topo.addr(c)
        return DstId(rid=rid, pnc=pid)

    comes = {t: (run[0], len(engs)) for c in sends for tr in sends[c] for run, cs, engs in tr if core in cs for t in run}

    def send_tiles(ready):
        n = 0
        for transfers in sends.get(core, []):
            for kind in "sc":
                tr = []
                for run, cs, engs in transfers:
                    ready(run, kind)
                    lo, hi = place[run[0]] * TC, (place[run[-1]] + 1) * TC
                    src = T.wsc[:, lo:hi] if kind == "s" else T.wq[:, lo:hi].bitcast(dt.uint8)
                    tr.append(RemoteDMATransfer(dst_ids=[dst_of(d) for d in cs], dma_engine_mask=bits(engs),
                                                remote_sem=S["%s%d" % (kind, run[0])], srcs=[src], dsts=[src] * len(cs)))
                    n += len(engs)
                g.remote_dma_fused(tr, local_sem=S.loc)
        return n

    seen = set()

    def once(queue, name, count):
        if (queue, name, count) not in seen:
            seen.add((queue, name, count))
            {"g": g, "p": g.tensor}[queue].wait_ge(S[name], count)

    if r is None:
        n = send_tiles(lambda run, kind: once("g", "%s%d" % (kind, comes[run[0]][0]), comes[run[0]][1]))
        g.wait_ge(S.loc, n)
        return

    V, A, P = g.vector, g.scalar, g.tensor
    copy = ActivationFunctionType.Copy
    make = make_all[r]
    order = sorted(range(NT), key=lambda t: (late[r][t], t))

    g.sync.dma_start(T.cws[:], T.cw[:, :]).then_inc(S.ldc, 16)
    A.dma_start(T.bk0[:], T.book[:, 0:1024]).then_inc(S.ldb0, 16)
    g.sync.dma_start(T.bk1[:], T.book[:, 1024:2048]).then_inc(S.ldb1, 16)
    g.sync.dma_start(T.xs[:], T.x[:, :]).then_inc(S.ldx, 16)

    V.wait_ge(S.ldc, 16)
    for t in range(4):
        V.tensor_scalar(T.off[:, :, t * LW:(t + 1) * LW], T.cws[:], 4, t, AluOpType.mult, AluOpType.add).then_inc(S.idx, 1)
        if t == 0:
            for u in range(2):
                V.tensor_scalar(T.snd[:, :, u * LW:(u + 1) * LW], T.cws[:, 2 * O - 2:2 * O, :], 4, u,
                                AluOpType.mult, AluOpType.add).then_inc(S.sidx, 1)

    asks = [d for d in range(NR) if d != r and O * r + O - 1 in make_all[d]]
    engs = topo.engines(core, T.cores[asks[0]])
    slots = [make_all[d].index(O * r + O - 1) - O for d in asks]
    g.wait_ge(S.sidx, 2)
    g.remote_dma_fused([RemoteDMATransfer(dst_ids=[dst_of(T.cores[d]) for d in asks], dma_engine_mask=bits(engs),
                                          remote_sem=S.larr, srcs=[T.snd[:]],
                                          dsts=[T.lof[:, 2 * f:2 * f + 2, :] for f in slots])], local_sem=S.loc)
    loc = len(engs)
    lists = sum(len(topo.engines(T.cores[t // O], core)) for t in make[O:])

    def offsets(k, m, t, n):
        if k < O:
            return T.off[:, 2 * k + m, t * LW:(t + n) * LW]
        return (T.lof, T.lof2)[t // 2][:, 2 * (k - O) + m, (t % 2) * LW:(t % 2 + n) * LW]

    where = {}
    ncp = {"s": 0, "v": 0}

    def copy_out(i, eng):
        bank, to = (i % 8) * 512, order[i] * TC
        ncp[eng] += 1
        if eng == "s":
            A.wait_ge(S.mm, i + 1)
            A.activation(T.ys[:, to:to + TC], T.ps[:, bank:bank + TC], copy).then_inc(S.cps, 1)
            where[i] = (S.cps, ncp[eng])
        else:
            V.wait_ge(S.mm, i + 1)
            V.tensor_copy(T.ys[:, to:to + TC], T.ps[:, bank:bank + TC]).then_inc(S.cpv, 1)
            where[i] = (S.cpv, ncp[eng])

    got = {}
    nsg = done = 0
    A.wait_ge(S.ldb0, 16)
    for k in range(NM):
        n = 1 if k == 0 else 4 if k < O else 2
        for t in range(0, 4, n):
            if k == 0:
                A.wait_ge(S.idx, t + 1)
            if k == O:
                A.wait_ge(*((S.larr, lists) if t == 0 else (S.lidx, 1)))
            A.activation(T["tmp%d" % k][:, t * TC:(t + n) * TC], T.bk0[:, 0:1024].indirect(offsets(k, 0, t, n)),
                         copy).then_inc(S.sg, 1)
            nsg += 1
            for u in range(t, t + n):
                got[k, u] = nsg
        for _ in range(S_COPIES.get(k, 0)):
            copy_out(done, "s")
            done += 1

    V.wait_ge(S.idx, 4)
    V.wait_ge(S.ldb1, 16)
    for k in range(NM):
        for t in range(4):
            if t == 0 or got[k, t] != got[k, t - 1]:
                V.wait_ge(S.sg, got[k, t])
            if k == O and t == 2:
                V.wait_ge(S.lidx, 1)
            V.tensor_tensor(T["w%d" % k][:, t:4 * TC:4], T.bk1[:, 0:1024].indirect(offsets(k, 1, t, 1)),
                            T["tmp%d" % k][:, t * TC:(t + 1) * TC], AluOpType.add).then_inc(S.vw, 1)
        if k == O - 1:
            V.wait_ge(S.larr, lists)
            V.tensor_scalar(T.lof2[:], T.lof[:], 2, None, AluOpType.add).then_inc(S.lidx, 1)
        V.wait_ge(S.vw, 4 * (k + 1))
        c = place[make[k]] * TC
        V.quantize_mx(T.wq[:, c:c + TC], T.wsc[:, c:c + TC], T["w%d" % k][:]).then_inc(S.vq, 1)
        if k == 0:
            V.wait_ge(S.ldx, 16)
            V.quantize_mx(T.xq[:], T.xsc[:], T.xs[:]).then_inc(S.xqd, 1)
    for n, i in enumerate(range(done, NT)):
        copy_out(i, "sv"[n % 2])

    P.wait_ge(S.xqd, 1)
    for i, t in enumerate(order):
        if t in make:
            P.wait_ge(S.vq, make.index(t) + 1)
        else:
            for kind in "sc":
                once("p", "%s%d" % (kind, comes[t][0]), comes[t][1])
        if i >= 8:
            P.wait_ge(*where[i - 8])
        c, bank = place[t] * TC, (i % 8) * 512
        P.matmul_mx(T.ps[:, bank:bank + TC], T.wq[:, c:c + TC], T.wsc[:, c:c + TC], T.xq[:], T.xsc[:],
                    True, True).then_inc(S.mm, 1)

    stores = []
    for t in order:
        if stores and stores[-1] == [t - 1]:
            stores[-1].append(t)
        else:
            stores.append([t])
    for run in stores:
        for t in run:
            g.sync.wait_ge(*where[order.index(t)])
        lo, hi = run[0] * TC, (run[-1] + 1) * TC
        g.sync.dma_start(T.y[:, lo:hi], T.ys[:, lo:hi]).then_inc(S.st, 16)
    g.sync.wait_ge(S.st, 16 * len(stores))

    loc += send_tiles(lambda run, kind: once("g", "vq", max(make.index(t) for t in run) + 1))
    g.wait_ge(S.loc, loc)
